import numpy as np
import ml_dtypes


def mxq(x, axis, fmt="e4m3"):
    dtype, down = {"e4m3": (ml_dtypes.float8_e4m3fn, 7), "e5m2": (ml_dtypes.float8_e5m2, 14)}[fmt]
    v = np.moveaxis(np.asarray(x, np.float32).astype(ml_dtypes.bfloat16).astype(np.float64), axis, -1)
    blocks = v.reshape(v.shape[:-1] + (-1, 32))
    amax = np.abs(blocks).max(-1, keepdims=True)
    byte = np.maximum(np.where(amax > 0, np.frexp(amax)[1] - 1 + 127, 0) - down, 1)
    scale = np.exp2(byte - 127.0)
    codes = (blocks / scale).astype(np.float32).astype(dtype).astype(np.float64)
    return np.moveaxis((codes * scale).reshape(v.shape), -1, axis)


WIDE = False


def mx_kscale(k):
    if not WIDE:
        return np.ones(k)
    levels = np.array([10, -10, 5, -5, 0])
    if k % 512:
        return np.exp2(np.random.permutation(np.resize(levels, k // 32))).repeat(32)
    a = np.empty((k // 512, 16))
    for p in range(k // 512):
        a[p, :8] = np.random.permutation(np.resize(levels, 8))
        for g in range(8):
            far = levels[np.abs(levels - a[p, g]) >= 10]
            a[p, g + 8] = far[np.random.randint(len(far))]
    return np.exp2(a.ravel()).repeat(32)


def f64(x):
    return np.asarray(x).astype(np.float64)


def striped(idx):
    return np.tile(idx.reshape(-1, 16).T, (8, 1)).astype(np.uint16)


def unstriped(offs):
    return offs[:16].T.reshape(-1).astype(np.int64)


def pack_weight(w):
    k, n = w.shape
    w = f64(np.asarray(w, np.float32).astype(ml_dtypes.bfloat16)).reshape(k // 32, 32, n)
    amax = np.abs(w).max(1)
    byte = np.clip(np.where(amax > 0, np.frexp(amax)[1] - 1 + 127 - 7, 1), 1, 254)
    scaled = (w * np.exp2(127.0 - byte)[:, None, :]).reshape(k, n).astype(np.float32)
    words = np.ascontiguousarray(scaled.reshape(k // 512, 128, 4, n).transpose(0, 1, 3, 2)).astype(ml_dtypes.float8_e4m3fn).view(np.uint8)
    return words, np.ascontiguousarray(byte.astype(np.uint8).reshape(k // 512, 16, n))


def unpack_weight(words, scales):
    g, p, n, _ = words.shape
    vals = np.ascontiguousarray(words).view(ml_dtypes.float8_e4m3fn).astype(np.float64) * np.repeat(np.exp2(scales.astype(np.float64) - 127.0), 8, axis=1)[..., None]
    return vals.transpose(0, 1, 3, 2).reshape(g * 512, n)


K, T, S, N, H = 1024, 2048, 512, 256, 512


def setup_inputs():
    n = np.random.standard_normal
    s = mx_kscale(K)[:, None]
    u = mx_kscale(H)
    packed_xT = pack_weight(n((K, T)) * s)
    return {
        "x_words": packed_xT[0],
        "x_scales": packed_xT[1],
        "w1": (n((K, H)) / np.sqrt(K) / s).astype(np.float32),
        "w2": (n((K, H)) / np.sqrt(K) / s).astype(np.float32),
        "ph": (np.random.uniform(-1.0, 1.0, (H, S))).astype(np.float32),
        "goal": (n((H, S))).astype(np.float32),
        "unit": (np.random.uniform(0.6, 1.4, (H, 1)) * u[:, None]).astype(np.float32),
        "w3": (n((H, N)) / np.sqrt(H) / u[:, None]).astype(np.float32),
        "offs": striped(np.random.permutation(T)[:S]),
        "phs": striped(np.random.permutation(S)),
    }


def reference(x_words, x_scales, w1, w2, ph, goal, unit, w3, offs, phs):
    xq = unpack_weight(x_words, x_scales)[:, unstriped(offs)]
    ww = mxq(f64(w2), 0, "e4m3").T @ xq
    ctr = np.tanh(ww)
    psi = np.exp(-1.0 * ((ctr - f64(ph)) ** 2))
    y = mxq(f64(w1), 0, "e4m3").T @ xq
    mps = psi.mean(axis=1, keepdims=True)
    force = (psi * y) / (mps + 0.2)
    fp = force[:, unstriped(phs)]
    acc_ = force + f64(goal) - (0.6 * fp)
    vel = acc_ / (np.abs(acc_) + 1.0)
    hid = f64(unit) * (vel + 0.3 * acc_)
    return mxq(f64(w3), 0, "e4m3").T @ mxq(hid, 0, "e4m3")

@@ -1,0 +1,263 @@
+from contextlib import ExitStack
+
+import concourse.mybir as mybir
+
+K, T, S, N, H = 1024, 2048, 512, 256, 512
+FLOPS = 2 * (2 * K * H * S) + 2 * H * N * S
+
+F32 = mybir.dt.float32
+BF16 = mybir.dt.bfloat16
+I32 = mybir.dt.int32
+U32 = mybir.dt.uint32
+U16 = mybir.dt.uint16
+U8 = mybir.dt.uint8
+FP8X4 = mybir.dt.float8_e4m3fn_x4
+ALU = mybir.AluOpType
+ACT = mybir.ActivationFunctionType
+
+P = 128
+PACK = 4
+PASSES = K // (P * PACK)
+HALVES = 2
+HALF = S // HALVES
+DAMP = 0.6
+
+
+def tile_picked_ydmpob_vel_p_kernel(tc, x_words, x_scales, w1, w2, ph, goal, unit, w3, offs, phs, out):
+    nc = tc.nc
+    with ExitStack() as ctx:
+        keep = ctx.enter_context(tc.tile_pool(name="keep", bufs=1))
+        psum = ctx.enter_context(tc.psum_pool(name="psum", bufs=1))
+
+        def sb(name, shape, dtype, tag=None):
+            return keep.tile(shape, dtype, name=name, tag=tag or name, align_bytes=64)
+
+        offs_sb = keep.tile([P, S // 16], U16, name="offs_sb")
+        phs_sb = keep.tile([P, S // 16], U16, name="phs_sb")
+
+        scale_table = sb("scale_table", [P, T], U8)
+        nc.vector.memset(scale_table[:].bitcast(I32), 0)
+
+        def load_words(g, pieces):
+            table = sb("word_table%d" % g, [P, T], U32)
+            words = x_words[g].rearrange("p n t -> p (n t)").bitcast(I32)
+            edges = [T * c // pieces // 64 * 64 for c in range(pieces + 1)]
+            for c in range(pieces):
+                cols = slice(edges[c], edges[c + 1])
+                nc.sync.dma_start(table[:, cols].bitcast(I32), words[:, cols])
+            return table
+
+        def load_weight(name, w, g, pieces):
+            rows = w[g * P * PACK : (g + 1) * P * PACK, :].rearrange("(p j) c -> p j c", j=PACK)
+            width = H // pieces
+            raws = []
+            for c in range(pieces):
+                raw = sb("%s_raw%d_%d" % (name, g, c), [P, PACK, width], F32)
+                nc.sync.dma_start(raw[:], rows[:, :, c * width : (c + 1) * width])
+                raws.append(raw)
+            return raws
+
+        def load_rows(name, src):
+            rows = src.rearrange("(p t) j -> p t j", t=PACK)
+            tiles = []
+            for pair in range(PACK // 2):
+                both = sb("%s%d" % (name, pair), [P, 2, S], F32)
+                nc.sync.dma_start(both[:], rows[:, 2 * pair : 2 * pair + 2, :])
+                tiles.extend([both[:, 0, :], both[:, 1, :]])
+            return tiles
+
+        nc.sync.dma_start(offs_sb[:], offs)
+        w2_raw = [load_weight("w2", w2, 0, 2)]
+        nc.sync.dma_start(phs_sb[:], phs)
+        unit_sb = sb("unit_sb", [P, PACK], F32)
+        nc.sync.dma_start(unit_sb[:], unit.rearrange("(p t) o -> p (t o)", t=PACK))
+        word_tables = [load_words(0, 3)]
+        for q in range(4):
+            nc.sync.dma_start(
+                scale_table[32 * q : 32 * q + 4 * PASSES, :].bitcast(I32),
+                x_scales[:, 4 * q : 4 * q + 4, :].bitcast(I32),
+            )
+        word_tables.append(load_words(1, 1))
+        w2_raw.append(load_weight("w2", w2, 1, 2))
+        ph_sb = load_rows("ph", ph)
+        w1_raw = [load_weight("w1", w1, 0, 1), load_weight("w1", w1, 1, 2)]
+        goal_sb = load_rows("goal", goal)
+        w3_raw = sb("w3_raw", [P, PACK, N], F32)
+        nc.sync.dma_start(w3_raw[:], w3.rearrange("(p j) n -> p j n", j=PACK))
+
+        x_codes = [sb("x_codes%d" % g, [P, S], U32) for g in range(PASSES)]
+        x_bytes = sb("x_bytes", [P, S], U8)
+
+        def deal(name, raws, g, scalar_share):
+            grouped = sb("%s_grouped%d" % (name, g), [P, PACK, P, PACK], BF16)
+            span = P // len(raws)
+            for c, raw in enumerate(raws):
+                src = raw[:].rearrange("p (a b) (m t) -> p m a t b", b=2, t=PACK)
+                dst = grouped[:, :, c * span : (c + 1) * span, :].rearrange("p t m (a b) -> p m a t b", b=2)
+                cut = span * scalar_share // 32 // 4 * 4
+                if cut:
+                    nc.scalar.copy(dst[:, :cut], src[:, :cut])
+                nc.vector.tensor_copy(dst[:, cut:], src[:, cut:])
+            return grouped
+
+        def quantize(name, grouped, words, calls):
+            codes = sb(name + "_codes", [P, words], U32)
+            scales = sb(name + "_scales", [P, words], U8)
+            step = words // calls
+            for c in range(calls):
+                cols = slice(c * step, (c + 1) * step)
+                nc.vector.quantize_mx(
+                    out=codes[:, cols].bitcast(FP8X4),
+                    scales=scales[:, cols],
+                    in_=grouped[:, c * step * PACK : (c + 1) * step * PACK],
+                )
+            return codes, scales
+
+        def flat(grouped):
+            return grouped[:].rearrange("p t m j -> p (t m j)")
+
+        def products(tag, quantized):
+            banks = [psum.tile([P, S], F32, name="%s%d" % (tag, t)) for t in range(PACK)]
+            for g in range(PASSES):
+                codes, scales = quantized[g]
+                for t in range(PACK):
+                    cols = slice(t * P, (t + 1) * P)
+                    nc.tensor.matmul_mx(
+                        out=banks[t][:],
+                        lhsT=codes[:, cols].bitcast(FP8X4),
+                        lhsT_scale=scales[:, cols],
+                        rhs=x_codes[g][:].bitcast(FP8X4),
+                        rhs_scale=x_bytes[4 * g : P, :],
+                        start=(g == 0),
+                        stop=(g == PASSES - 1),
+                    )
+            return banks
+
+        w2_q = [quantize("w2_0", flat(deal("w2", w2_raw[0], 0, 12)), H, 1)]
+        nc.vector.tensor_copy(x_codes[0][:], word_tables[0][:].indirect(offs_sb[:]))
+        nc.vector.tensor_copy(x_bytes[:], scale_table[:].indirect(offs_sb[:]))
+        nc.vector.tensor_copy(x_codes[1][:], word_tables[1][:].indirect(offs_sb[:]))
+        w2_q.append(quantize("w2_1", flat(deal("w2", w2_raw[1], 1, 12)), H, PACK))
+        ww = products("ww", w2_q)
+
+        ctr, diff, dist, psi = [[sb("%s%d" % (name, t), [P, S], F32) for t in range(PACK)] for name in ("ctr", "diff", "dist", "psi")]
+        total = sb("total", [P, PACK], F32)
+        for t in range(PACK):
+            nc.scalar.activation(ctr[t][:], ww[t][:], ACT.Tanh)
+            nc.vector.tensor_tensor(diff[t][:], ctr[t][:], ph_sb[t], ALU.subtract)
+        for t in range(PACK):
+            nc.scalar.activation(dist[t][:], diff[t][:], ACT.Square)
+            nc.scalar.activation(psi[t][:], dist[t][:], ACT.Exp, scale=-1.0, accum_out=total[:, t : t + 1])
+
+        w1_q = [quantize("w1_0", flat(deal("w1", w1_raw[0], 0, 0)), H, 1)]
+        w1_q.append(quantize("w1_1", flat(deal("w1", w1_raw[1], 1, 0)), H, PACK))
+        y = products("y", w1_q)
+
+        denom = sb("denom", [P, PACK], F32, tag="w1_grouped1")
+        gain = sb("gain", [P, PACK], F32)
+
+        def normalise(ts):
+            nc.vector.tensor_scalar(denom[:, ts], total[:, ts], -1.0 / (DAMP * S), -0.2 / DAMP, ALU.mult, ALU.add)
+            nc.vector.reciprocal(gain[:, ts], denom[:, ts])
+
+        unit_lin = sb("unit_lin", [P, PACK], F32)
+        nc.vector.tensor_scalar(unit_lin[:], unit_sb[:], 0.3, None, ALU.mult)
+
+        w3_grouped = sb("w3_grouped", [P, N, PACK], BF16)
+        nc.scalar.copy(
+            w3_grouped[:].rearrange("p (c i) j -> p c j i", i=4),
+            w3_raw[:].rearrange("p j (c i) -> p c j i", i=4),
+        )
+        w3_codes, w3_scales = quantize("w3", w3_grouped[:].rearrange("p n j -> p (n j)"), N, 1)
+
+        def planes(name, dtype):
+            return [sb("%s%d" % (name, h), [P, PACK, HALF], dtype) for h in range(HALVES)]
+
+        acc, size, square, recip, slope = [planes(name, F32) for name in ("acc", "size", "square", "recip", "slope")]
+        hid = planes("hid", BF16)
+        damping = [sb("damping%d" % t, [P, S], F32) for t in range(PACK)]
+        pull = [sb("pull%d" % t, [P, S], F32) for t in range(PACK)]
+
+        def force(t):
+            nc.vector.scalar_tensor_tensor(damping[t][:], psi[t][:], gain[:, t : t + 1], y[t][:], ALU.mult, ALU.mult)
+
+        def add_goal(t):
+            nc.vector.scalar_tensor_tensor(pull[t][:], damping[t][:], -1.0 / DAMP, goal_sb[t], ALU.mult, ALU.add)
+
+        def couple(t, h):
+            picked = damping[t][:].indirect(phs_sb[:, h * HALF // 16 : (h + 1) * HALF // 16])
+            nc.vector.tensor_tensor(acc[h][:, t, :], picked, pull[t][:, h * HALF : (h + 1) * HALF], ALU.add)
+
+        def saturate(ts, h):
+            nc.scalar.activation(size[h][:, ts, :], acc[h][:, ts, :], ACT.Abs)
+            nc.scalar.activation(square[h][:, ts, :], size[h][:, ts, :], ACT.Square, bias=1.0)
+            nc.scalar.activation(recip[h][:, ts, :], square[h][:, ts, :], ACT.Abs_reciprocal_sqrt)
+
+        def scale(t, h):
+            col = slice(t, t + 1)
+            if h == 0:
+                nc.scalar.activation(slope[h][:, t, :], recip[h][:, t, :], ACT.Identity, bias=unit_lin[:, col], scale=unit_sb[:, col])
+            else:
+                nc.vector.tensor_scalar(slope[h][:, t, :], recip[h][:, t, :], unit_sb[:, col], unit_lin[:, col], ALU.mult, ALU.add)
+
+        def finish(ts, h):
+            nc.vector.tensor_tensor(hid[h][:, ts, :], slope[h][:, ts, :], acc[h][:, ts, :], ALU.mult)
+
+        def project(h):
+            cols = slice(h * HALF, (h + 1) * HALF)
+            hid_grouped = sb("hid_grouped%d" % h, [P, HALF, PACK], BF16)
+            dst = hid_grouped[:].rearrange("p (c i) t -> p c t i", i=4)
+            src = hid[h][:].rearrange("p t (c i) -> p c t i", i=4)
+            cut = HALF // 4 if h == 0 else 16
+            nc.scalar.copy(dst[:, :cut], src[:, :cut])
+            if cut < HALF // 4:
+                nc.vector.tensor_copy(dst[:, cut:], src[:, cut:])
+            hid_codes, hid_scales = quantize("hid%d" % h, hid_grouped[:].rearrange("p n t -> p (n t)"), HALF, 1)
+            result = sb("result%d" % h, [P, N // P, HALF], F32)
+            for m in range(N // P):
+                bank = psum.tile([P, S], F32, name="ww%d" % (h * (N // P) + m))
+                rows = slice(m * P, (m + 1) * P)
+                nc.tensor.matmul_mx(
+                    out=bank[:, :HALF],
+                    lhsT=w3_codes[:, rows].bitcast(FP8X4),
+                    lhsT_scale=w3_scales[:, rows],
+                    rhs=hid_codes[:].bitcast(FP8X4),
+                    rhs_scale=hid_scales[:],
+                    start=True,
+                    stop=True,
+                )
+                if m == 0:
+                    nc.scalar.copy(result[:, m, :], bank[:, :HALF])
+                else:
+                    nc.vector.tensor_copy(result[:, m, :], bank[:, :HALF])
+            nc.sync.dma_start(out.rearrange("(m p) j -> p m j", p=P)[:, :, cols], result[:])
+
+        def one(t):
+            return slice(t, t + 1)
+
+        normalise(slice(0, 2))
+        force(0)
+        force(1)
+        add_goal(0)
+        normalise(slice(2, 4))
+        for t in range(PACK):
+            couple(t, 0)
+            if t + 1 < PACK:
+                add_goal(t + 1)
+            if t + 2 < PACK:
+                force(t + 2)
+            saturate(one(t), 0)
+            scale(t, 0)
+        for t in range(PACK):
+            couple(t, 1)
+        saturate(slice(0, 2), 1)
+        saturate(one(2), 1)
+        saturate(one(3), 1)
+        finish(slice(0, 2), 0)
+        finish(slice(2, 4), 0)
+        project(0)
+        for t in range(0, PACK, 2):
+            scale(t, 1)
+            scale(t + 1, 1)
+            finish(slice(t, t + 2), 1)
+        project(1)

@@ -38,14 +38,10 @@ def tile_picked_ydmpob_vel_p_kernel(tc, x_words, x_scales, w1, w2, ph, goal, uni
         scale_table = sb("scale_table", [P, T], U8)
         nc.vector.memset(scale_table[:].bitcast(I32), 0)
 
-        def load_words(g, pieces):
-            table = sb("word_table%d" % g, [P, T], U32)
+        def load_words(g, first, last):
             words = x_words[g].rearrange("p n t -> p (n t)").bitcast(I32)
-            edges = [T * c // pieces // 64 * 64 for c in range(pieces + 1)]
-            for c in range(pieces):
-                cols = slice(edges[c], edges[c + 1])
-                nc.sync.dma_start(table[:, cols].bitcast(I32), words[:, cols])
-            return table
+            cols = slice(first * T // 4, last * T // 4)
+            nc.sync.dma_start(word_tables[g][:, cols].bitcast(I32), words[:, cols])
 
         def load_weight(name, w, g, pieces):
             rows = w[g * P * PACK : (g + 1) * P * PACK, :].rearrange("(p j) c -> p j c", j=PACK)
@@ -67,54 +63,71 @@ def tile_picked_ydmpob_vel_p_kernel(tc, x_words, x_scales, w1, w2, ph, goal, uni
             return tiles
 
         nc.sync.dma_start(offs_sb[:], offs)
-        w2_raw = [load_weight("w2", w2, 0, 2)]
+        first = sb("w2_raw0_0", [P, PACK, H], F32)
+        first_rows = w2[: P * PACK, :].rearrange("(p j) c -> p j c", j=PACK)
+        nc.sync.dma_start(first[:, :2, :], first_rows[:, :2, :])
         nc.sync.dma_start(phs_sb[:], phs)
         unit_sb = sb("unit_sb", [P, PACK], F32)
         nc.sync.dma_start(unit_sb[:], unit.rearrange("(p t) o -> p (t o)", t=PACK))
-        word_tables = [load_words(0, 3)]
+        nc.sync.dma_start(first[:, 2:, :], first_rows[:, 2:, :])
+        w2_raw = [[first]]
+        word_tables = [sb("word_table%d" % g, [P, T], U32) for g in range(PASSES)]
+        load_words(0, 0, 2)
+        load_words(0, 2, 3)
+        load_words(0, 3, 4)
         for q in range(4):
             nc.sync.dma_start(
                 scale_table[32 * q : 32 * q + 4 * PASSES, :].bitcast(I32),
                 x_scales[:, 4 * q : 4 * q + 4, :].bitcast(I32),
             )
-        word_tables.append(load_words(1, 1))
-        w2_raw.append(load_weight("w2", w2, 1, 2))
+        load_words(1, 0, 4)
+        w2_raw.append(load_weight("w2", w2, 1, 1))
+        w1_raw = [load_weight("w1", w1, 0, 1)]
         ph_sb = load_rows("ph", ph)
-        w1_raw = [load_weight("w1", w1, 0, 1), load_weight("w1", w1, 1, 2)]
+        w1_raw.append(load_weight("w1", w1, 1, 2))
         goal_sb = load_rows("goal", goal)
         w3_raw = sb("w3_raw", [P, PACK, N], F32)
         nc.sync.dma_start(w3_raw[:], w3.rearrange("(p j) n -> p j n", j=PACK))
 
+        unit_lin = sb("unit_lin", [P, PACK], F32)
+        nc.scalar.activation(unit_lin[:], unit_sb[:], ACT.Copy, scale=0.3)
+
         x_codes = [sb("x_codes%d" % g, [P, S], U32) for g in range(PASSES)]
         x_bytes = sb("x_bytes", [P, S], U8)
 
-        def deal(name, raws, g, scalar_share):
+        def quantize(codes, scales, grouped, cols):
+            nc.vector.quantize_mx(
+                out=codes[:, cols].bitcast(FP8X4),
+                scales=scales[:, cols],
+                in_=grouped[:, cols.start * PACK : cols.stop * PACK],
+            )
+
+        def operand(name, words):
+            return sb(name + "_codes", [P, words], U32), sb(name + "_scales", [P, words], U8)
+
+        def deal(grouped, raw, c, span, pairs, scalar_cols):
+            src = raw[:].rearrange("p j (m a b) -> p a m j b", a=2, b=2)[:, pairs]
+            dst = grouped[:, :, c * span : (c + 1) * span, :].rearrange("p (a b) m j -> p a m j b", b=2)[:, pairs]
+            if scalar_cols:
+                nc.scalar.copy(dst[:, :, :scalar_cols], src[:, :, :scalar_cols])
+            nc.vector.tensor_copy(dst[:, :, scalar_cols:], src[:, :, scalar_cols:])
+
+        def prepare(name, raws, g, scalar_cols):
             grouped = sb("%s_grouped%d" % (name, g), [P, PACK, P, PACK], BF16)
+            flat = grouped[:].rearrange("p t m j -> p (t m j)")
+            codes, scales = operand("%s_%d" % (name, g), H)
             span = P // len(raws)
-            for c, raw in enumerate(raws):
-                src = raw[:].rearrange("p (a b) (m t) -> p m a t b", b=2, t=PACK)
-                dst = grouped[:, :, c * span : (c + 1) * span, :].rearrange("p t m (a b) -> p m a t b", b=2)
-                cut = span * scalar_share // 32 // 4 * 4
-                if cut:
-                    nc.scalar.copy(dst[:, :cut], src[:, :cut])
-                nc.vector.tensor_copy(dst[:, cut:], src[:, cut:])
-            return grouped
-
-        def quantize(name, grouped, words, calls):
-            codes = sb(name + "_codes", [P, words], U32)
-            scales = sb(name + "_scales", [P, words], U8)
-            step = words // calls
-            for c in range(calls):
-                cols = slice(c * step, (c + 1) * step)
-                nc.vector.quantize_mx(
-                    out=codes[:, cols].bitcast(FP8X4),
-                    scales=scales[:, cols],
-                    in_=grouped[:, c * step * PACK : (c + 1) * step * PACK],
-                )
+            if g < PASSES - 1:
+                deal(grouped, raws[0], 0, span, slice(0, 2), scalar_cols)
+                quantize(codes, scales, flat, slice(0, H))
+                return codes, scales
+            for c, raw in enumerate(raws[:-1]):
+                deal(grouped, raw, c, span, slice(0, 2), scalar_cols)
+            for a in range(2):
+                deal(grouped, raws[-1], len(raws) - 1, span, slice(a, a + 1), scalar_cols)
+            for t in range(PACK):
+                quantize(codes, scales, flat, slice(t * P, (t + 1) * P))
             return codes, scales
-
-        def flat(grouped):
-            return grouped[:].rearrange("p t m j -> p (t m j)")
 
         def products(tag, quantized):
             banks = [psum.tile([P, S], F32, name="%s%d" % (tag, t)) for t in range(PACK)]
@@ -133,86 +146,104 @@ def tile_picked_ydmpob_vel_p_kernel(tc, x_words, x_scales, w1, w2, ph, goal, uni
                     )
             return banks
 
-        w2_q = [quantize("w2_0", flat(deal("w2", w2_raw[0], 0, 12)), H, 1)]
+        w2_q = [prepare("w2", w2_raw[0], 0, 48)]
         nc.vector.tensor_copy(x_codes[0][:], word_tables[0][:].indirect(offs_sb[:]))
         nc.vector.tensor_copy(x_bytes[:], scale_table[:].indirect(offs_sb[:]))
         nc.vector.tensor_copy(x_codes[1][:], word_tables[1][:].indirect(offs_sb[:]))
-        w2_q.append(quantize("w2_1", flat(deal("w2", w2_raw[1], 1, 12)), H, PACK))
+        w2_q.append(prepare("w2", w2_raw[1], 1, 48))
         ww = products("ww", w2_q)
 
-        ctr, diff, dist, psi = [[sb("%s%d" % (name, t), [P, S], F32) for t in range(PACK)] for name in ("ctr", "diff", "dist", "psi")]
+        ctr, diff, dist = [[sb("%s%d" % (name, t), [P, S], F32) for t in range(PACK)] for name in ("ctr", "diff", "dist")]
+        window = [sb("window%d" % t, [P, 2 * S], F32) for t in range(PACK)]
+        force = [tile[:, :S] for tile in window]
+        psi = [tile[:, S:] for tile in window]
         total = sb("total", [P, PACK], F32)
         for t in range(PACK):
             nc.scalar.activation(ctr[t][:], ww[t][:], ACT.Tanh)
             nc.vector.tensor_tensor(diff[t][:], ctr[t][:], ph_sb[t], ALU.subtract)
         for t in range(PACK):
             nc.scalar.activation(dist[t][:], diff[t][:], ACT.Square)
-            nc.scalar.activation(psi[t][:], dist[t][:], ACT.Exp, scale=-1.0, accum_out=total[:, t : t + 1])
+            nc.scalar.activation(psi[t], dist[t][:], ACT.Exp, scale=-1.0, accum_out=total[:, t : t + 1])
 
-        w1_q = [quantize("w1_0", flat(deal("w1", w1_raw[0], 0, 0)), H, 1)]
-        w1_q.append(quantize("w1_1", flat(deal("w1", w1_raw[1], 1, 0)), H, PACK))
+        w1_q = [prepare("w1", w1_raw[g], g, 0) for g in range(PASSES)]
         y = products("y", w1_q)
 
-        denom = sb("denom", [P, PACK], F32, tag="w1_grouped1")
         gain = sb("gain", [P, PACK], F32)
+        early, late = slice(0, 2), slice(2, 4)
+        denom = sb("denom", [P, 2], F32, tag="w1_grouped1")
+        nc.vector.tensor_scalar(denom[:], total[:, early], -1.0 / (DAMP * S), -0.2 / DAMP, ALU.mult, ALU.add)
+        nc.vector.reciprocal(gain[:, early], denom[:])
+        denom_sq = sb("denom_sq", [P, 2], F32)
+        nc.scalar.activation(denom_sq[:], total[:, late], ACT.Square, bias=0.2, scale=1.0 / S)
+        late_gain = sb("late_gain", [P, 2], F32)
+        nc.scalar.activation(late_gain[:], denom_sq[:], ACT.Abs_reciprocal_sqrt)
+        nc.vector.tensor_tensor(gain[:, late], late_gain[:], unit_sb[:, late], ALU.mult)
+        unit_safe = sb("unit_safe", [P, PACK], F32)
+        nc.vector.scalar_tensor_tensor(unit_safe[:], unit_sb[:], 0.0, unit_sb[:], ALU.is_equal, ALU.add)
+        unit_inv = sb("unit_inv", [P, PACK], F32)
+        nc.vector.reciprocal(unit_inv[:], unit_safe[:])
 
-        def normalise(ts):
-            nc.vector.tensor_scalar(denom[:, ts], total[:, ts], -1.0 / (DAMP * S), -0.2 / DAMP, ALU.mult, ALU.add)
-            nc.vector.reciprocal(gain[:, ts], denom[:, ts])
-
-        unit_lin = sb("unit_lin", [P, PACK], F32)
-        nc.vector.tensor_scalar(unit_lin[:], unit_sb[:], 0.3, None, ALU.mult)
 
         w3_grouped = sb("w3_grouped", [P, N, PACK], BF16)
         nc.scalar.copy(
             w3_grouped[:].rearrange("p (c i) j -> p c j i", i=4),
             w3_raw[:].rearrange("p j (c i) -> p c j i", i=4),
         )
-        w3_codes, w3_scales = quantize("w3", w3_grouped[:].rearrange("p n j -> p (n j)"), N, 1)
+        w3_codes, w3_scales = operand("w3", N)
+        quantize(w3_codes, w3_scales, w3_grouped[:].rearrange("p n j -> p (n j)"), slice(0, N))
 
-        def planes(name, dtype):
-            return [sb("%s%d" % (name, h), [P, PACK, HALF], dtype) for h in range(HALVES)]
+        pull, fetched, acc, size, root, slope = [
+            sb(name, [P, PACK, S], F32) for name in ("pull", "fetched", "acc", "size", "root", "slope")
+        ]
+        hid = sb("hid", [P, PACK, S], BF16)
 
-        acc, size, square, recip, slope = [planes(name, F32) for name in ("acc", "size", "square", "recip", "slope")]
-        hid = planes("hid", BF16)
-        damping = [sb("damping%d" % t, [P, S], F32) for t in range(PACK)]
-        pull = [sb("pull%d" % t, [P, S], F32) for t in range(PACK)]
+        def picked(t, cols):
+            return window[t][:].indirect(phs_sb[:, cols.start // 16 : cols.stop // 16])
 
-        def force(t):
-            nc.vector.scalar_tensor_tensor(damping[t][:], psi[t][:], gain[:, t : t + 1], y[t][:], ALU.mult, ALU.mult)
+        def weigh(t):
+            nc.vector.scalar_tensor_tensor(force[t], psi[t], gain[:, t : t + 1], y[t][:], ALU.mult, ALU.mult)
 
-        def add_goal(t):
-            nc.vector.scalar_tensor_tensor(pull[t][:], damping[t][:], -1.0 / DAMP, goal_sb[t], ALU.mult, ALU.add)
+        def early_goal(t):
+            nc.vector.scalar_tensor_tensor(pull[:, t, :], force[t], -1.0 / DAMP, goal_sb[t], ALU.mult, ALU.add)
 
-        def couple(t, h):
-            picked = damping[t][:].indirect(phs_sb[:, h * HALF // 16 : (h + 1) * HALF // 16])
-            nc.vector.tensor_tensor(acc[h][:, t, :], picked, pull[t][:, h * HALF : (h + 1) * HALF], ALU.add)
+        def early_damp(t):
+            nc.vector.tensor_tensor(acc[:, t, :], picked(t, whole), pull[:, t, :], ALU.add)
+            nc.scalar.activation(size[:, t, :], acc[:, t, :], ACT.Abs)
+            nc.scalar.activation(root[:, t, :], size[:, t, :], ACT.Abs_reciprocal_sqrt, bias=1.0)
 
-        def saturate(ts, h):
-            nc.scalar.activation(size[h][:, ts, :], acc[h][:, ts, :], ACT.Abs)
-            nc.scalar.activation(square[h][:, ts, :], size[h][:, ts, :], ACT.Square, bias=1.0)
-            nc.scalar.activation(recip[h][:, ts, :], square[h][:, ts, :], ACT.Abs_reciprocal_sqrt)
+        def early_scale(t):
+            nc.vector.scalar_tensor_tensor(slope[:, t, :], root[:, t, :], unit_sb[:, t : t + 1], root[:, t, :], ALU.mult, ALU.mult)
 
-        def scale(t, h):
-            col = slice(t, t + 1)
-            if h == 0:
-                nc.scalar.activation(slope[h][:, t, :], recip[h][:, t, :], ACT.Identity, bias=unit_lin[:, col], scale=unit_sb[:, col])
-            else:
-                nc.vector.tensor_scalar(slope[h][:, t, :], recip[h][:, t, :], unit_sb[:, col], unit_lin[:, col], ALU.mult, ALU.add)
+        def early_finish(t):
+            nc.vector.scalar_tensor_tensor(hid[:, t, :], slope[:, t, :], unit_lin[:, t : t + 1], acc[:, t, :], ALU.add, ALU.mult)
 
-        def finish(ts, h):
-            nc.vector.tensor_tensor(hid[h][:, ts, :], slope[h][:, ts, :], acc[h][:, ts, :], ALU.mult)
+        def late_goal(t):
+            nc.vector.scalar_tensor_tensor(pull[:, t, :], goal_sb[t], unit_sb[:, t : t + 1], force[t], ALU.mult, ALU.add)
+
+        def late_fetch(t):
+            nc.scalar.activation(fetched[:, t, :], picked(t, whole), ACT.Copy)
+
+        def late_damp(ts, cols):
+            nc.vector.scalar_tensor_tensor(acc[:, ts, cols], fetched[:, ts, cols], -DAMP, pull[:, ts, cols], ALU.mult, ALU.add)
+            for t in range(ts.start, ts.stop):
+                nc.scalar.activation(size[:, t, cols], acc[:, t, cols], ACT.Abs, scale=unit_inv[:, t : t + 1])
+            nc.scalar.activation(root[:, ts, cols], size[:, ts, cols], ACT.Square, bias=1.0)
+            nc.scalar.activation(slope[:, ts, cols], root[:, ts, cols], ACT.Abs_reciprocal_sqrt)
+
+        def late_finish(ts, cols):
+            nc.vector.scalar_tensor_tensor(hid[:, ts, cols], slope[:, ts, cols], 0.3, acc[:, ts, cols], ALU.add, ALU.mult)
 
         def project(h):
             cols = slice(h * HALF, (h + 1) * HALF)
             hid_grouped = sb("hid_grouped%d" % h, [P, HALF, PACK], BF16)
             dst = hid_grouped[:].rearrange("p (c i) t -> p c t i", i=4)
-            src = hid[h][:].rearrange("p t (c i) -> p c t i", i=4)
-            cut = HALF // 4 if h == 0 else 16
-            nc.scalar.copy(dst[:, :cut], src[:, :cut])
-            if cut < HALF // 4:
-                nc.vector.tensor_copy(dst[:, cut:], src[:, cut:])
-            hid_codes, hid_scales = quantize("hid%d" % h, hid_grouped[:].rearrange("p n t -> p (n t)"), HALF, 1)
+            src = hid[:, :, cols].rearrange("p t (c i) -> p c t i", i=4)
+            cut = 0 if h == 0 else 24
+            if cut:
+                nc.scalar.copy(dst[:, :cut], src[:, :cut])
+            nc.vector.tensor_copy(dst[:, cut:], src[:, cut:])
+            hid_codes, hid_scales = operand("hid%d" % h, HALF)
+            quantize(hid_codes, hid_scales, hid_grouped[:].rearrange("p n t -> p (n t)"), slice(0, HALF))
             result = sb("result%d" % h, [P, N // P, HALF], F32)
             for m in range(N // P):
                 bank = psum.tile([P, S], F32, name="ww%d" % (h * (N // P) + m))
@@ -232,32 +263,28 @@ def tile_picked_ydmpob_vel_p_kernel(tc, x_words, x_scales, w1, w2, ph, goal, uni
                     nc.vector.tensor_copy(result[:, m, :], bank[:, :HALF])
             nc.sync.dma_start(out.rearrange("(m p) j -> p m j", p=P)[:, :, cols], result[:])
 
-        def one(t):
-            return slice(t, t + 1)
-
-        normalise(slice(0, 2))
-        force(0)
-        force(1)
-        add_goal(0)
-        normalise(slice(2, 4))
-        for t in range(PACK):
-            couple(t, 0)
-            if t + 1 < PACK:
-                add_goal(t + 1)
-            if t + 2 < PACK:
-                force(t + 2)
-            saturate(one(t), 0)
-            scale(t, 0)
-        for t in range(PACK):
-            couple(t, 1)
-        saturate(slice(0, 2), 1)
-        saturate(one(2), 1)
-        saturate(one(3), 1)
-        finish(slice(0, 2), 0)
-        finish(slice(2, 4), 0)
+        whole, lo, hi = slice(0, S), slice(0, HALF), slice(HALF, S)
+        weigh(0)
+        weigh(1)
+        early_goal(0)
+        early_goal(1)
+        early_damp(0)
+        weigh(2)
+        late_fetch(2)
+        weigh(3)
+        late_fetch(3)
+        early_damp(1)
+        late_goal(2)
+        late_goal(3)
+        late_damp(late, lo)
+        early_scale(0)
+        late_damp(slice(2, 3), hi)
+        late_damp(slice(3, 4), hi)
+        early_scale(1)
+        early_finish(0)
+        early_finish(1)
+        late_finish(late, lo)
+        late_finish(slice(2, 3), hi)
         project(0)
-        for t in range(0, PACK, 2):
-            scale(t, 1)
-            scale(t + 1, 1)
-            finish(slice(t, t + 2), 1)
+        late_finish(slice(3, 4), hi)
         project(1)

@@ -21,6 +21,9 @@ PASSES = K // (P * PACK)
 HALVES = 2
 HALF = S // HALVES
 DAMP = 0.6
+SPLIT = 256
+LO_SHARE = 256
+HI_SHARE = 96
 
 
 def tile_picked_ydmpob_vel_p_kernel(tc, x_words, x_scales, w1, w2, ph, goal, unit, w3, offs, phs, out):
@@ -62,14 +65,11 @@ def tile_picked_ydmpob_vel_p_kernel(tc, x_words, x_scales, w1, w2, ph, goal, uni
                 tiles.extend([both[:, 0, :], both[:, 1, :]])
             return tiles
 
-        nc.sync.dma_start(offs_sb[:], offs)
         first = sb("w2_raw0_0", [P, PACK, H], F32)
         first_rows = w2[: P * PACK, :].rearrange("(p j) c -> p j c", j=PACK)
-        nc.sync.dma_start(first[:, :2, :], first_rows[:, :2, :])
-        nc.sync.dma_start(phs_sb[:], phs)
-        unit_sb = sb("unit_sb", [P, PACK], F32)
-        nc.sync.dma_start(unit_sb[:], unit.rearrange("(p t) o -> p (t o)", t=PACK))
-        nc.sync.dma_start(first[:, 2:, :], first_rows[:, 2:, :])
+        for j in range(PACK):
+            nc.sync.dma_start(first[:, j, :], first_rows[:, j, :])
+        nc.sync.dma_start(offs_sb[:], offs)
         w2_raw = [[first]]
         word_tables = [sb("word_table%d" % g, [P, T], U32) for g in range(PASSES)]
         load_words(0, 0, 2)
@@ -84,13 +84,13 @@ def tile_picked_ydmpob_vel_p_kernel(tc, x_words, x_scales, w1, w2, ph, goal, uni
         w2_raw.append(load_weight("w2", w2, 1, 1))
         w1_raw = [load_weight("w1", w1, 0, 1)]
         ph_sb = load_rows("ph", ph)
+        unit_sb = sb("unit_sb", [P, PACK], F32)
+        nc.sync.dma_start(unit_sb[:], unit.rearrange("(p t) o -> p (t o)", t=PACK))
         w1_raw.append(load_weight("w1", w1, 1, 2))
+        nc.sync.dma_start(phs_sb[:], phs)
         goal_sb = load_rows("goal", goal)
         w3_raw = sb("w3_raw", [P, PACK, N], F32)
         nc.sync.dma_start(w3_raw[:], w3.rearrange("(p j) n -> p j n", j=PACK))
-
-        unit_lin = sb("unit_lin", [P, PACK], F32)
-        nc.scalar.activation(unit_lin[:], unit_sb[:], ACT.Copy, scale=0.3)
 
         x_codes = [sb("x_codes%d" % g, [P, S], U32) for g in range(PASSES)]
         x_bytes = sb("x_bytes", [P, S], U8)
@@ -102,8 +102,8 @@ def tile_picked_ydmpob_vel_p_kernel(tc, x_words, x_scales, w1, w2, ph, goal, uni
                 in_=grouped[:, cols.start * PACK : cols.stop * PACK],
             )
 
-        def operand(name, words):
-            return sb(name + "_codes", [P, words], U32), sb(name + "_scales", [P, words], U8)
+        def operand(name, words, tag=None):
+            return sb(name + "_codes", [P, words], U32, tag), sb(name + "_scales", [P, words], U8)
 
         def deal(grouped, raw, c, span, pairs, scalar_cols):
             src = raw[:].rearrange("p j (m a b) -> p a m j b", a=2, b=2)[:, pairs]
@@ -112,7 +112,7 @@ def tile_picked_ydmpob_vel_p_kernel(tc, x_words, x_scales, w1, w2, ph, goal, uni
                 nc.scalar.copy(dst[:, :, :scalar_cols], src[:, :, :scalar_cols])
             nc.vector.tensor_copy(dst[:, :, scalar_cols:], src[:, :, scalar_cols:])
 
-        def prepare(name, raws, g, scalar_cols):
+        def prepare(name, raws, g, scalar_cols, between=()):
             grouped = sb("%s_grouped%d" % (name, g), [P, PACK, P, PACK], BF16)
             flat = grouped[:].rearrange("p t m j -> p (t m j)")
             codes, scales = operand("%s_%d" % (name, g), H)
@@ -123,9 +123,11 @@ def tile_picked_ydmpob_vel_p_kernel(tc, x_words, x_scales, w1, w2, ph, goal, uni
                 return codes, scales
             for c, raw in enumerate(raws[:-1]):
                 deal(grouped, raw, c, span, slice(0, 2), scalar_cols)
-            for a in range(2):
-                deal(grouped, raws[-1], len(raws) - 1, span, slice(a, a + 1), scalar_cols)
             for t in range(PACK):
+                if t % 2 == 0:
+                    deal(grouped, raws[-1], len(raws) - 1, span, slice(t // 2, t // 2 + 1), scalar_cols)
+                if t < len(between):
+                    between[t]()
                 quantize(codes, scales, flat, slice(t * P, (t + 1) * P))
             return codes, scales
 
@@ -146,7 +148,7 @@ def tile_picked_ydmpob_vel_p_kernel(tc, x_words, x_scales, w1, w2, ph, goal, uni
                     )
             return banks
 
-        w2_q = [prepare("w2", w2_raw[0], 0, 48)]
+        w2_q = [prepare("w2", w2_raw[0], 0, 0)]
         nc.vector.tensor_copy(x_codes[0][:], word_tables[0][:].indirect(offs_sb[:]))
         nc.vector.tensor_copy(x_bytes[:], scale_table[:].indirect(offs_sb[:]))
         nc.vector.tensor_copy(x_codes[1][:], word_tables[1][:].indirect(offs_sb[:]))
@@ -158,39 +160,43 @@ def tile_picked_ydmpob_vel_p_kernel(tc, x_words, x_scales, w1, w2, ph, goal, uni
         force = [tile[:, :S] for tile in window]
         psi = [tile[:, S:] for tile in window]
         total = sb("total", [P, PACK], F32)
+        w1_q = []
         for t in range(PACK):
+            if t == 2:
+                w1_q.append(prepare("w1", w1_raw[0], 0, 0))
             nc.scalar.activation(ctr[t][:], ww[t][:], ACT.Tanh)
             nc.vector.tensor_tensor(diff[t][:], ctr[t][:], ph_sb[t], ALU.subtract)
         for t in range(PACK):
             nc.scalar.activation(dist[t][:], diff[t][:], ACT.Square)
             nc.scalar.activation(psi[t], dist[t][:], ACT.Exp, scale=-1.0, accum_out=total[:, t : t + 1])
 
-        w1_q = [prepare("w1", w1_raw[g], g, 0) for g in range(PASSES)]
-        y = products("y", w1_q)
-
-        gain = sb("gain", [P, PACK], F32)
         early, late = slice(0, 2), slice(2, 4)
-        denom = sb("denom", [P, 2], F32, tag="w1_grouped1")
-        nc.vector.tensor_scalar(denom[:], total[:, early], -1.0 / (DAMP * S), -0.2 / DAMP, ALU.mult, ALU.add)
-        nc.vector.reciprocal(gain[:, early], denom[:])
-        denom_sq = sb("denom_sq", [P, 2], F32)
-        nc.scalar.activation(denom_sq[:], total[:, late], ACT.Square, bias=0.2, scale=1.0 / S)
-        late_gain = sb("late_gain", [P, 2], F32)
-        nc.scalar.activation(late_gain[:], denom_sq[:], ACT.Abs_reciprocal_sqrt)
-        nc.vector.tensor_tensor(gain[:, late], late_gain[:], unit_sb[:, late], ALU.mult)
-        unit_safe = sb("unit_safe", [P, PACK], F32)
-        nc.vector.scalar_tensor_tensor(unit_safe[:], unit_sb[:], 0.0, unit_sb[:], ALU.is_equal, ALU.add)
-        unit_inv = sb("unit_inv", [P, PACK], F32)
+        unit_neg = sb("unit_neg", [P, 2, 2], F32)
+        nc.vector.tensor_scalar(unit_neg[:, 0, :], unit_sb[:, late], -1.0, None, ALU.mult)
+        nc.vector.tensor_scalar(unit_neg[:, 1, :], unit_sb[:, late], -0.3, None, ALU.mult)
+        unit_safe = sb("unit_safe", [P, 2], F32)
+        nc.vector.scalar_tensor_tensor(unit_safe[:], unit_sb[:, early], 0.0, unit_sb[:, early], ALU.is_equal, ALU.add)
+        unit_inv = sb("unit_inv", [P, 2], F32)
         nc.vector.reciprocal(unit_inv[:], unit_safe[:])
 
-
-        w3_grouped = sb("w3_grouped", [P, N, PACK], BF16)
-        nc.scalar.copy(
-            w3_grouped[:].rearrange("p (c i) j -> p c j i", i=4),
-            w3_raw[:].rearrange("p j (c i) -> p c j i", i=4),
+        denom = sb("denom", [P, 2], F32)
+        plain_gain = sb("plain_gain", [P, 2], F32)
+        early_gain = sb("early_gain", [P, 2], F32)
+        gain_steps = (
+            lambda: nc.vector.tensor_scalar(denom[:], total[:, early], 1.0 / S, 0.2, ALU.mult, ALU.add),
+            lambda: nc.vector.reciprocal(plain_gain[:], denom[:]),
+            lambda: nc.vector.tensor_tensor(early_gain[:], plain_gain[:], unit_sb[:, early], ALU.mult),
         )
-        w3_codes, w3_scales = operand("w3", N)
-        quantize(w3_codes, w3_scales, w3_grouped[:].rearrange("p n j -> p (n j)"), slice(0, N))
+        w1_q.append(prepare("w1", w1_raw[1], 1, 0, gain_steps))
+        y = products("y", w1_q)
+
+        late_gain = sb("late_gain", [P, 2], F32)
+        third_denom = sb("third_denom", [P, 1], F32)
+        denom_sq = sb("denom_sq", [P, 1], F32)
+        nc.scalar.activation(denom_sq[:], total[:, 3:4], ACT.Square, bias=0.2 / DAMP, scale=1.0 / (DAMP * S))
+        last_gain = sb("last_gain", [P, 1], F32)
+        nc.scalar.activation(last_gain[:], denom_sq[:], ACT.Abs_reciprocal_sqrt)
+        gain = [early_gain[:, 0:1], early_gain[:, 1:2], late_gain[:, 0:1], last_gain[:]]
 
         pull, fetched, acc, size, root, slope = [
             sb(name, [P, PACK, S], F32) for name in ("pull", "fetched", "acc", "size", "root", "slope")
@@ -201,90 +207,105 @@ def tile_picked_ydmpob_vel_p_kernel(tc, x_words, x_scales, w1, w2, ph, goal, uni
             return window[t][:].indirect(phs_sb[:, cols.start // 16 : cols.stop // 16])
 
         def weigh(t):
-            nc.vector.scalar_tensor_tensor(force[t], psi[t], gain[:, t : t + 1], y[t][:], ALU.mult, ALU.mult)
+            nc.vector.scalar_tensor_tensor(force[t], psi[t], gain[t], y[t][:], ALU.mult, ALU.mult)
 
         def early_goal(t):
-            nc.vector.scalar_tensor_tensor(pull[:, t, :], force[t], -1.0 / DAMP, goal_sb[t], ALU.mult, ALU.add)
-
-        def early_damp(t):
-            nc.vector.tensor_tensor(acc[:, t, :], picked(t, whole), pull[:, t, :], ALU.add)
-            nc.scalar.activation(size[:, t, :], acc[:, t, :], ACT.Abs)
-            nc.scalar.activation(root[:, t, :], size[:, t, :], ACT.Abs_reciprocal_sqrt, bias=1.0)
-
-        def early_scale(t):
-            nc.vector.scalar_tensor_tensor(slope[:, t, :], root[:, t, :], unit_sb[:, t : t + 1], root[:, t, :], ALU.mult, ALU.mult)
-
-        def early_finish(t):
-            nc.vector.scalar_tensor_tensor(hid[:, t, :], slope[:, t, :], unit_lin[:, t : t + 1], acc[:, t, :], ALU.add, ALU.mult)
-
-        def late_goal(t):
             nc.vector.scalar_tensor_tensor(pull[:, t, :], goal_sb[t], unit_sb[:, t : t + 1], force[t], ALU.mult, ALU.add)
 
-        def late_fetch(t):
+        def early_fetch(t):
             nc.scalar.activation(fetched[:, t, :], picked(t, whole), ACT.Copy)
 
-        def late_damp(ts, cols):
-            nc.vector.scalar_tensor_tensor(acc[:, ts, cols], fetched[:, ts, cols], -DAMP, pull[:, ts, cols], ALU.mult, ALU.add)
-            for t in range(ts.start, ts.stop):
-                nc.scalar.activation(size[:, t, cols], acc[:, t, cols], ACT.Abs, scale=unit_inv[:, t : t + 1])
-            nc.scalar.activation(root[:, ts, cols], size[:, ts, cols], ACT.Square, bias=1.0)
-            nc.scalar.activation(slope[:, ts, cols], root[:, ts, cols], ACT.Abs_reciprocal_sqrt)
+        def early_damp(t):
+            nc.vector.scalar_tensor_tensor(acc[:, t, :], fetched[:, t, :], -DAMP, pull[:, t, :], ALU.mult, ALU.add)
+            nc.scalar.activation(size[:, t, :], acc[:, t, :], ACT.Abs, scale=unit_inv[:, t : t + 1])
+            nc.scalar.activation(root[:, t, :], size[:, t, :], ACT.Square, bias=1.0)
+            nc.scalar.activation(slope[:, t, :], root[:, t, :], ACT.Abs_reciprocal_sqrt)
 
-        def late_finish(ts, cols):
-            nc.vector.scalar_tensor_tensor(hid[:, ts, cols], slope[:, ts, cols], 0.3, acc[:, ts, cols], ALU.add, ALU.mult)
+        def early_finish(t, cols):
+            nc.vector.scalar_tensor_tensor(hid[:, t, cols], slope[:, t, cols], 0.3, acc[:, t, cols], ALU.add, ALU.mult)
 
-        def project(h):
-            cols = slice(h * HALF, (h + 1) * HALF)
-            hid_grouped = sb("hid_grouped%d" % h, [P, HALF, PACK], BF16)
+        def late_goal(t):
+            nc.vector.scalar_tensor_tensor(pull[:, t, :], force[t], 1.0 / DAMP, goal_sb[t], ALU.mult, ALU.add)
+
+        def late_damp(t, cols):
+            nc.vector.tensor_tensor(acc[:, t, cols], picked(t, cols), pull[:, t, cols], ALU.subtract)
+            nc.scalar.activation(size[:, t, cols], acc[:, t, cols], ACT.Abs)
+            nc.scalar.activation(root[:, t, cols], size[:, t, cols], ACT.Abs_reciprocal_sqrt, bias=1.0)
+
+        def late_scale(t, cols):
+            nc.vector.scalar_tensor_tensor(slope[:, t, cols], root[:, t, cols], unit_neg[:, 0, t - 2 : t - 1], root[:, t, cols], ALU.mult, ALU.mult)
+
+        def late_finish(t, cols):
+            nc.vector.scalar_tensor_tensor(hid[:, t, cols], slope[:, t, cols], unit_neg[:, 1, t - 2 : t - 1], acc[:, t, cols], ALU.add, ALU.mult)
+
+        def project(h, cols, scalar_cols):
+            width = cols.stop - cols.start
+            hid_grouped = sb("hid_grouped%d" % h, [P, width, PACK], BF16)
             dst = hid_grouped[:].rearrange("p (c i) t -> p c t i", i=4)
             src = hid[:, :, cols].rearrange("p t (c i) -> p c t i", i=4)
-            cut = 0 if h == 0 else 24
+            cut = scalar_cols // 4
             if cut:
                 nc.scalar.copy(dst[:, :cut], src[:, :cut])
-            nc.vector.tensor_copy(dst[:, cut:], src[:, cut:])
-            hid_codes, hid_scales = operand("hid%d" % h, HALF)
-            quantize(hid_codes, hid_scales, hid_grouped[:].rearrange("p n t -> p (n t)"), slice(0, HALF))
-            result = sb("result%d" % h, [P, N // P, HALF], F32)
+            if scalar_cols < width:
+                nc.vector.tensor_copy(dst[:, cut:], src[:, cut:])
+            hid_codes, hid_scales = operand("hid%d" % h, width)
+            quantize(hid_codes, hid_scales, hid_grouped[:].rearrange("p n t -> p (n t)"), slice(0, width))
+            result = sb("result%d" % h, [P, N // P, width], F32)
             for m in range(N // P):
                 bank = psum.tile([P, S], F32, name="ww%d" % (h * (N // P) + m))
                 rows = slice(m * P, (m + 1) * P)
-                nc.tensor.matmul_mx(
-                    out=bank[:, :HALF],
-                    lhsT=w3_codes[:, rows].bitcast(FP8X4),
-                    lhsT_scale=w3_scales[:, rows],
-                    rhs=hid_codes[:].bitcast(FP8X4),
-                    rhs_scale=hid_scales[:],
-                    start=True,
-                    stop=True,
-                )
+                for start in range(0, width, HALF):
+                    part = slice(start, min(start + HALF, width))
+                    nc.tensor.matmul_mx(
+                        out=bank[:, part],
+                        lhsT=w3_codes[:, rows].bitcast(FP8X4),
+                        lhsT_scale=w3_scales[:, rows],
+                        rhs=hid_codes[:, part].bitcast(FP8X4),
+                        rhs_scale=hid_scales[:, part],
+                        start=True,
+                        stop=True,
+                    )
                 if m == 0:
-                    nc.scalar.copy(result[:, m, :], bank[:, :HALF])
+                    nc.scalar.copy(result[:, m, :], bank[:, :width])
                 else:
-                    nc.vector.tensor_copy(result[:, m, :], bank[:, :HALF])
-            nc.sync.dma_start(out.rearrange("(m p) j -> p m j", p=P)[:, :, cols], result[:])
+                    nc.vector.tensor_copy(result[:, m, :], bank[:, :width])
+                nc.sync.dma_start(out[rows, cols], result[:, m, :])
 
-        whole, lo, hi = slice(0, S), slice(0, HALF), slice(HALF, S)
+        whole, lo, hi = slice(0, S), slice(0, SPLIT), slice(SPLIT, S)
         weigh(0)
         weigh(1)
+        nc.vector.tensor_scalar(third_denom[:], total[:, 2:3], 1.0 / (DAMP * S), 0.2 / DAMP, ALU.mult, ALU.add)
+        nc.vector.reciprocal(late_gain[:, 0:1], third_denom[:])
+        early_fetch(0)
+        early_fetch(1)
         early_goal(0)
-        early_goal(1)
-        early_damp(0)
         weigh(2)
-        late_fetch(2)
-        weigh(3)
-        late_fetch(3)
-        early_damp(1)
+        early_goal(1)
         late_goal(2)
+        early_damp(0)
+        late_damp(2, whole)
+        weigh(3)
+        early_damp(1)
         late_goal(3)
-        late_damp(late, lo)
-        early_scale(0)
-        late_damp(slice(2, 3), hi)
-        late_damp(slice(3, 4), hi)
-        early_scale(1)
-        early_finish(0)
-        early_finish(1)
-        late_finish(late, lo)
-        late_finish(slice(2, 3), hi)
-        project(0)
-        late_finish(slice(3, 4), hi)
-        project(1)
+        late_damp(3, lo)
+        late_damp(3, hi)
+        late_scale(2, whole)
+        early_finish(0, lo)
+        late_scale(3, lo)
+        late_finish(2, lo)
+        early_finish(1, lo)
+        late_finish(3, lo)
+        w3_grouped = sb("w3_grouped", [P, N, PACK], BF16, tag="pull")
+        nc.vector.tensor_copy(
+            w3_grouped[:].rearrange("p (c i) j -> p c j i", i=4),
+            w3_raw[:].rearrange("p j (c i) -> p c j i", i=4),
+        )
+        w3_codes, w3_scales = operand("w3", N)
+        quantize(w3_codes, w3_scales, w3_grouped[:].rearrange("p n j -> p (n j)"), slice(0, N))
+        early_finish(0, hi)
+        late_finish(2, hi)
+        late_scale(3, hi)
+        early_finish(1, hi)
+        late_finish(3, hi)
+        project(0, lo, LO_SHARE)
+        project(1, hi, HI_SHARE)

from contextlib import ExitStack

import concourse.mybir as mybir

K, T, S, N, H = 1024, 2048, 512, 256, 512
FLOPS = 2 * (2 * K * H * S) + 2 * H * N * S

F32 = mybir.dt.float32
BF16 = mybir.dt.bfloat16
I32 = mybir.dt.int32
U32 = mybir.dt.uint32
U16 = mybir.dt.uint16
U8 = mybir.dt.uint8
FP8X4 = mybir.dt.float8_e4m3fn_x4
ALU = mybir.AluOpType
ACT = mybir.ActivationFunctionType

P = 128
PACK = 4
PASSES = K // (P * PACK)
HALVES = 2
HALF = S // HALVES
DAMP = 0.6
SPLIT = 256
LO_SHARE = 256
HI_SHARE = 96


def tile_picked_ydmpob_vel_p_kernel(tc, x_words, x_scales, w1, w2, ph, goal, unit, w3, offs, phs, out):
    nc = tc.nc
    with ExitStack() as ctx:
        keep = ctx.enter_context(tc.tile_pool(name="keep", bufs=1))
        psum = ctx.enter_context(tc.psum_pool(name="psum", bufs=1))

        def sb(name, shape, dtype, tag=None):
            return keep.tile(shape, dtype, name=name, tag=tag or name, align_bytes=64)

        offs_sb = keep.tile([P, S // 16], U16, name="offs_sb")
        phs_sb = keep.tile([P, S // 16], U16, name="phs_sb")

        scale_table = sb("scale_table", [P, T], U8)
        nc.vector.memset(scale_table[:].bitcast(I32), 0)

        def load_words(g, first, last):
            words = x_words[g].rearrange("p n t -> p (n t)").bitcast(I32)
            cols = slice(first * T // 4, last * T // 4)
            nc.sync.dma_start(word_tables[g][:, cols].bitcast(I32), words[:, cols])

        def load_weight(name, w, g, pieces):
            rows = w[g * P * PACK : (g + 1) * P * PACK, :].rearrange("(p j) c -> p j c", j=PACK)
            width = H // pieces
            raws = []
            for c in range(pieces):
                raw = sb("%s_raw%d_%d" % (name, g, c), [P, PACK, width], F32)
                nc.sync.dma_start(raw[:], rows[:, :, c * width : (c + 1) * width])
                raws.append(raw)
            return raws

        def load_rows(name, src):
            rows = src.rearrange("(p t) j -> p t j", t=PACK)
            tiles = []
            for pair in range(PACK // 2):
                both = sb("%s%d" % (name, pair), [P, 2, S], F32)
                nc.sync.dma_start(both[:], rows[:, 2 * pair : 2 * pair + 2, :])
                tiles.extend([both[:, 0, :], both[:, 1, :]])
            return tiles

        first = sb("w2_raw0_0", [P, PACK, H], F32)
        first_rows = w2[: P * PACK, :].rearrange("(p j) c -> p j c", j=PACK)
        for j in range(PACK):
            nc.sync.dma_start(first[:, j, :], first_rows[:, j, :])
        nc.sync.dma_start(offs_sb[:], offs)
        w2_raw = [[first]]
        word_tables = [sb("word_table%d" % g, [P, T], U32) for g in range(PASSES)]
        load_words(0, 0, 2)
        load_words(0, 2, 3)
        load_words(0, 3, 4)
        for q in range(4):
            nc.sync.dma_start(
                scale_table[32 * q : 32 * q + 4 * PASSES, :].bitcast(I32),
                x_scales[:, 4 * q : 4 * q + 4, :].bitcast(I32),
            )
        load_words(1, 0, 4)
        w2_raw.append(load_weight("w2", w2, 1, 1))
        w1_raw = [load_weight("w1", w1, 0, 1)]
        ph_sb = load_rows("ph", ph)
        unit_sb = sb("unit_sb", [P, PACK], F32)
        nc.sync.dma_start(unit_sb[:], unit.rearrange("(p t) o -> p (t o)", t=PACK))
        w1_raw.append(load_weight("w1", w1, 1, 2))
        nc.sync.dma_start(phs_sb[:], phs)
        goal_sb = load_rows("goal", goal)
        w3_raw = sb("w3_raw", [P, PACK, N], F32)
        nc.sync.dma_start(w3_raw[:], w3.rearrange("(p j) n -> p j n", j=PACK))

        x_codes = [sb("x_codes%d" % g, [P, S], U32) for g in range(PASSES)]
        x_bytes = sb("x_bytes", [P, S], U8)

        def quantize(codes, scales, grouped, cols):
            nc.vector.quantize_mx(
                out=codes[:, cols].bitcast(FP8X4),
                scales=scales[:, cols],
                in_=grouped[:, cols.start * PACK : cols.stop * PACK],
            )

        def operand(name, words, tag=None):
            return sb(name + "_codes", [P, words], U32, tag), sb(name + "_scales", [P, words], U8)

        def deal(grouped, raw, c, span, pairs, scalar_cols):
            src = raw[:].rearrange("p j (m a b) -> p a m j b", a=2, b=2)[:, pairs]
            dst = grouped[:, :, c * span : (c + 1) * span, :].rearrange("p (a b) m j -> p a m j b", b=2)[:, pairs]
            if scalar_cols:
                nc.scalar.copy(dst[:, :, :scalar_cols], src[:, :, :scalar_cols])
            nc.vector.tensor_copy(dst[:, :, scalar_cols:], src[:, :, scalar_cols:])

        def prepare(name, raws, g, scalar_cols, between=()):
            grouped = sb("%s_grouped%d" % (name, g), [P, PACK, P, PACK], BF16)
            flat = grouped[:].rearrange("p t m j -> p (t m j)")
            codes, scales = operand("%s_%d" % (name, g), H)
            span = P // len(raws)
            if g < PASSES - 1:
                deal(grouped, raws[0], 0, span, slice(0, 2), scalar_cols)
                quantize(codes, scales, flat, slice(0, H))
                return codes, scales
            for c, raw in enumerate(raws[:-1]):
                deal(grouped, raw, c, span, slice(0, 2), scalar_cols)
            for t in range(PACK):
                if t % 2 == 0:
                    deal(grouped, raws[-1], len(raws) - 1, span, slice(t // 2, t // 2 + 1), scalar_cols)
                if t < len(between):
                    between[t]()
                quantize(codes, scales, flat, slice(t * P, (t + 1) * P))
            return codes, scales

        def products(tag, quantized):
            banks = [psum.tile([P, S], F32, name="%s%d" % (tag, t)) for t in range(PACK)]
            for g in range(PASSES):
                codes, scales = quantized[g]
                for t in range(PACK):
                    cols = slice(t * P, (t + 1) * P)
                    nc.tensor.matmul_mx(
                        out=banks[t][:],
                        lhsT=codes[:, cols].bitcast(FP8X4),
                        lhsT_scale=scales[:, cols],
                        rhs=x_codes[g][:].bitcast(FP8X4),
                        rhs_scale=x_bytes[4 * g : P, :],
                        start=(g == 0),
                        stop=(g == PASSES - 1),
                    )
            return banks

        w2_q = [prepare("w2", w2_raw[0], 0, 0)]
        nc.vector.tensor_copy(x_codes[0][:], word_tables[0][:].indirect(offs_sb[:]))
        nc.vector.tensor_copy(x_bytes[:], scale_table[:].indirect(offs_sb[:]))
        nc.vector.tensor_copy(x_codes[1][:], word_tables[1][:].indirect(offs_sb[:]))
        w2_q.append(prepare("w2", w2_raw[1], 1, 48))
        ww = products("ww", w2_q)

        ctr, diff, dist = [[sb("%s%d" % (name, t), [P, S], F32) for t in range(PACK)] for name in ("ctr", "diff", "dist")]
        window = [sb("window%d" % t, [P, 2 * S], F32) for t in range(PACK)]
        force = [tile[:, :S] for tile in window]
        psi = [tile[:, S:] for tile in window]
        total = sb("total", [P, PACK], F32)
        w1_q = []
        for t in range(PACK):
            if t == 2:
                w1_q.append(prepare("w1", w1_raw[0], 0, 0))
            nc.scalar.activation(ctr[t][:], ww[t][:], ACT.Tanh)
            nc.vector.tensor_tensor(diff[t][:], ctr[t][:], ph_sb[t], ALU.subtract)
        for t in range(PACK):
            nc.scalar.activation(dist[t][:], diff[t][:], ACT.Square)
            nc.scalar.activation(psi[t], dist[t][:], ACT.Exp, scale=-1.0, accum_out=total[:, t : t + 1])

        early, late = slice(0, 2), slice(2, 4)
        unit_neg = sb("unit_neg", [P, 2, 2], F32)
        nc.vector.tensor_scalar(unit_neg[:, 0, :], unit_sb[:, late], -1.0, None, ALU.mult)
        nc.vector.tensor_scalar(unit_neg[:, 1, :], unit_sb[:, late], -0.3, None, ALU.mult)
        unit_safe = sb("unit_safe", [P, 2], F32)
        nc.vector.scalar_tensor_tensor(unit_safe[:], unit_sb[:, early], 0.0, unit_sb[:, early], ALU.is_equal, ALU.add)
        unit_inv = sb("unit_inv", [P, 2], F32)
        nc.vector.reciprocal(unit_inv[:], unit_safe[:])

        denom = sb("denom", [P, 2], F32)
        plain_gain = sb("plain_gain", [P, 2], F32)
        early_gain = sb("early_gain", [P, 2], F32)
        gain_steps = (
            lambda: nc.vector.tensor_scalar(denom[:], total[:, early], 1.0 / S, 0.2, ALU.mult, ALU.add),
            lambda: nc.vector.reciprocal(plain_gain[:], denom[:]),
            lambda: nc.vector.tensor_tensor(early_gain[:], plain_gain[:], unit_sb[:, early], ALU.mult),
        )
        w1_q.append(prepare("w1", w1_raw[1], 1, 0, gain_steps))
        y = products("y", w1_q)

        late_gain = sb("late_gain", [P, 2], F32)
        third_denom = sb("third_denom", [P, 1], F32)
        denom_sq = sb("denom_sq", [P, 1], F32)
        nc.scalar.activation(denom_sq[:], total[:, 3:4], ACT.Square, bias=0.2 / DAMP, scale=1.0 / (DAMP * S))
        last_gain = sb("last_gain", [P, 1], F32)
        nc.scalar.activation(last_gain[:], denom_sq[:], ACT.Abs_reciprocal_sqrt)
        gain = [early_gain[:, 0:1], early_gain[:, 1:2], late_gain[:, 0:1], last_gain[:]]

        pull, fetched, acc, size, root, slope = [
            sb(name, [P, PACK, S], F32) for name in ("pull", "fetched", "acc", "size", "root", "slope")
        ]
        hid = sb("hid", [P, PACK, S], BF16)

        def picked(t, cols):
            return window[t][:].indirect(phs_sb[:, cols.start // 16 : cols.stop // 16])

        def weigh(t):
            nc.vector.scalar_tensor_tensor(force[t], psi[t], gain[t], y[t][:], ALU.mult, ALU.mult)

        def early_goal(t):
            nc.vector.scalar_tensor_tensor(pull[:, t, :], goal_sb[t], unit_sb[:, t : t + 1], force[t], ALU.mult, ALU.add)

        def early_fetch(t):
            nc.scalar.activation(fetched[:, t, :], picked(t, whole), ACT.Copy)

        def early_damp(t):
            nc.vector.scalar_tensor_tensor(acc[:, t, :], fetched[:, t, :], -DAMP, pull[:, t, :], ALU.mult, ALU.add)
            nc.scalar.activation(size[:, t, :], acc[:, t, :], ACT.Abs, scale=unit_inv[:, t : t + 1])
            nc.scalar.activation(root[:, t, :], size[:, t, :], ACT.Square, bias=1.0)
            nc.scalar.activation(slope[:, t, :], root[:, t, :], ACT.Abs_reciprocal_sqrt)

        def early_finish(t, cols):
            nc.vector.scalar_tensor_tensor(hid[:, t, cols], slope[:, t, cols], 0.3, acc[:, t, cols], ALU.add, ALU.mult)

        def late_goal(t):
            nc.vector.scalar_tensor_tensor(pull[:, t, :], force[t], 1.0 / DAMP, goal_sb[t], ALU.mult, ALU.add)

        def late_damp(t, cols):
            nc.vector.tensor_tensor(acc[:, t, cols], picked(t, cols), pull[:, t, cols], ALU.subtract)
            nc.scalar.activation(size[:, t, cols], acc[:, t, cols], ACT.Abs)
            nc.scalar.activation(root[:, t, cols], size[:, t, cols], ACT.Abs_reciprocal_sqrt, bias=1.0)

        def late_scale(t, cols):
            nc.vector.scalar_tensor_tensor(slope[:, t, cols], root[:, t, cols], unit_neg[:, 0, t - 2 : t - 1], root[:, t, cols], ALU.mult, ALU.mult)

        def late_finish(t, cols):
            nc.vector.scalar_tensor_tensor(hid[:, t, cols], slope[:, t, cols], unit_neg[:, 1, t - 2 : t - 1], acc[:, t, cols], ALU.add, ALU.mult)

        def project(h, cols, scalar_cols):
            width = cols.stop - cols.start
            hid_grouped = sb("hid_grouped%d" % h, [P, width, PACK], BF16)
            dst = hid_grouped[:].rearrange("p (c i) t -> p c t i", i=4)
            src = hid[:, :, cols].rearrange("p t (c i) -> p c t i", i=4)
            cut = scalar_cols // 4
            if cut:
                nc.scalar.copy(dst[:, :cut], src[:, :cut])
            if scalar_cols < width:
                nc.vector.tensor_copy(dst[:, cut:], src[:, cut:])
            hid_codes, hid_scales = operand("hid%d" % h, width)
            quantize(hid_codes, hid_scales, hid_grouped[:].rearrange("p n t -> p (n t)"), slice(0, width))
            result = sb("result%d" % h, [P, N // P, width], F32)
            for m in range(N // P):
                bank = psum.tile([P, S], F32, name="ww%d" % (h * (N // P) + m))
                rows = slice(m * P, (m + 1) * P)
                for start in range(0, width, HALF):
                    part = slice(start, min(start + HALF, width))
                    nc.tensor.matmul_mx(
                        out=bank[:, part],
                        lhsT=w3_codes[:, rows].bitcast(FP8X4),
                        lhsT_scale=w3_scales[:, rows],
                        rhs=hid_codes[:, part].bitcast(FP8X4),
                        rhs_scale=hid_scales[:, part],
                        start=True,
                        stop=True,
                    )
                if m == 0:
                    nc.scalar.copy(result[:, m, :], bank[:, :width])
                else:
                    nc.vector.tensor_copy(result[:, m, :], bank[:, :width])
                nc.sync.dma_start(out[rows, cols], result[:, m, :])

        whole, lo, hi = slice(0, S), slice(0, SPLIT), slice(SPLIT, S)
        weigh(0)
        weigh(1)
        nc.vector.tensor_scalar(third_denom[:], total[:, 2:3], 1.0 / (DAMP * S), 0.2 / DAMP, ALU.mult, ALU.add)
        nc.vector.reciprocal(late_gain[:, 0:1], third_denom[:])
        early_fetch(0)
        early_fetch(1)
        early_goal(0)
        weigh(2)
        early_goal(1)
        late_goal(2)
        early_damp(0)
        late_damp(2, whole)
        weigh(3)
        early_damp(1)
        late_goal(3)
        late_damp(3, lo)
        late_damp(3, hi)
        late_scale(2, whole)
        early_finish(0, lo)
        late_scale(3, lo)
        late_finish(2, lo)
        early_finish(1, lo)
        late_finish(3, lo)
        w3_grouped = sb("w3_grouped", [P, N, PACK], BF16, tag="pull")
        nc.vector.tensor_copy(
            w3_grouped[:].rearrange("p (c i) j -> p c j i", i=4),
            w3_raw[:].rearrange("p j (c i) -> p c j i", i=4),
        )
        w3_codes, w3_scales = operand("w3", N)
        quantize(w3_codes, w3_scales, w3_grouped[:].rearrange("p n j -> p (n j)"), slice(0, N))
        early_finish(0, hi)
        late_finish(2, hi)
        late_scale(3, hi)
        early_finish(1, hi)
        late_finish(3, hi)
        project(0, lo, LO_SHARE)
        project(1, hi, HI_SHARE)
